import numpy as np
import ml_dtypes

BF16 = ml_dtypes.bfloat16


def bf(x):
    return np.asarray(x, np.float32).astype(BF16)


def f32(x):
    return np.asarray(x, np.float32)


def f64(x):
    return np.asarray(x).astype(np.float64)


def striped(idx):
    return np.tile(idx.reshape(-1, 16).T, (8, 1))


S, K, M, N = 512, 128, 512, 384


def setup_inputs():
    return {"base": bf(np.random.standard_normal((M, S))), "x": bf(np.random.standard_normal((K, N))), "w": bf(np.random.standard_normal((K, M)) / np.sqrt(K)), "s": f32(0.5 + np.random.random_sample((M, 1))), "b": f32(0.5 * np.random.standard_normal((M, 1))), "offs": striped(np.random.permutation(S)[:N])}


def reference(base, x, w, s, b, offs):
    idx = offs[:16].T.reshape(-1)
    z = f64(base).copy()
    z[:, idx] += f64(w).T @ f64(x)
    return z * f64(s) + f64(b)

@@ -1,0 +1,79 @@
+import concourse.mybir as mybir
+from concourse.masks import make_identity
+
+BF16 = mybir.dt.bfloat16
+F32 = mybir.dt.float32
+U16 = mybir.dt.uint16
+
+P = 128
+M = 512
+S = 512
+N = 384
+BLOCKS = M // P
+
+FLOPS = 2 * P * M * N
+
+
+def tile_scatter_matmul_kernel(tc, base, x, w, s, b, offs, out):
+    nc = tc.nc
+    base_blocks = base.rearrange("(a p) t -> a p t", p=P)
+    out_blocks = out.rearrange("(a p) t -> a p t", p=P)
+
+    with (
+        tc.tile_pool(name="held", bufs=1) as held,
+        tc.psum_pool(name="psum", bufs=1) as psum,
+    ):
+        offsets = held.tile([P, N // 16], U16, name="offsets")
+        nc.sync.dma_start(offsets[:], offs)
+
+        base_tiles = [held.tile([P, S], BF16, name=f"base{a}") for a in range(BLOCKS)]
+        for a in range(BLOCKS):
+            queue = nc.sync if a % 2 == 0 else nc.scalar
+            queue.dma_start(base_tiles[a][:], base_blocks[a])
+
+        ident = held.tile([P, P], BF16, name="ident")
+        make_identity(nc, ident[:])
+        x_tile = held.tile([P, N], BF16, name="x_tile")
+        nc.gpsimd.dma_start(x_tile[:], x)
+        w_tile = held.tile([P, M], BF16, name="w_tile")
+        nc.gpsimd.dma_start(w_tile[:], w)
+
+        gain = held.tile([P, BLOCKS], F32, name="gain")
+        shift = held.tile([P, BLOCKS], F32, name="shift")
+        with nc.allow_non_contiguous_dma(reason="one float32 to a partition, 4 columns"):
+            nc.scalar.dma_start(gain[:], s.rearrange("(a p) o -> p (a o)", p=P))
+            nc.scalar.dma_start(shift[:], b.rearrange("(a p) o -> p (a o)", p=P))
+
+        windows = [psum.tile([P, S], F32, name=f"window{a}") for a in range(BLOCKS)]
+        for a in range(BLOCKS):
+            nc.tensor.matmul(windows[a][:], ident[:], base_tiles[a][:], start=True, stop=False)
+
+        for a in range(BLOCKS):
+            nc.tensor.matmul(
+                windows[a][:].indirect(offsets[:]),
+                w_tile[:, a * P : (a + 1) * P],
+                x_tile[:],
+                start=False,
+                stop=True,
+            )
+
+        for a in range(BLOCKS):
+            result = held.tile([P, S], F32, name=f"result{a}")
+            if a % 2 == 0:
+                nc.vector.tensor_scalar(
+                    result[:],
+                    windows[a][:],
+                    gain[:, a : a + 1],
+                    shift[:, a : a + 1],
+                    mybir.AluOpType.mult,
+                    mybir.AluOpType.add,
+                )
+            else:
+                nc.scalar.activation(
+                    result[:],
+                    windows[a][:],
+                    mybir.ActivationFunctionType.Identity,
+                    bias=shift[:, a : a + 1],
+                    scale=gain[:, a : a + 1],
+                )
+            nc.sync.dma_start(out_blocks[a], result[:])

@@ -10,6 +10,7 @@ M = 512
 S = 512
 N = 384
 BLOCKS = M // P
+HALF = S // 2
 
 FLOPS = 2 * P * M * N
 
@@ -30,19 +31,19 @@ def tile_scatter_matmul_kernel(tc, base, x, w, s, b, offs, out):
         for a in range(BLOCKS):
             queue = nc.sync if a % 2 == 0 else nc.scalar
             queue.dma_start(base_tiles[a][:], base_blocks[a])
-
-        ident = held.tile([P, P], BF16, name="ident")
-        make_identity(nc, ident[:])
         x_tile = held.tile([P, N], BF16, name="x_tile")
-        nc.gpsimd.dma_start(x_tile[:], x)
+        nc.sync.dma_start(x_tile[:], x)
         w_tile = held.tile([P, M], BF16, name="w_tile")
-        nc.gpsimd.dma_start(w_tile[:], w)
+        nc.scalar.dma_start(w_tile[:], w)
 
         gain = held.tile([P, BLOCKS], F32, name="gain")
         shift = held.tile([P, BLOCKS], F32, name="shift")
         with nc.allow_non_contiguous_dma(reason="one float32 to a partition, 4 columns"):
-            nc.scalar.dma_start(gain[:], s.rearrange("(a p) o -> p (a o)", p=P))
+            nc.sync.dma_start(gain[:], s.rearrange("(a p) o -> p (a o)", p=P))
             nc.scalar.dma_start(shift[:], b.rearrange("(a p) o -> p (a o)", p=P))
+
+        ident = held.tile([P, P], BF16, name="ident")
+        make_identity(nc, ident[:])
 
         windows = [psum.tile([P, S], F32, name=f"window{a}") for a in range(BLOCKS)]
         for a in range(BLOCKS):
@@ -59,21 +60,15 @@ def tile_scatter_matmul_kernel(tc, base, x, w, s, b, offs, out):
 
         for a in range(BLOCKS):
             result = held.tile([P, S], F32, name=f"result{a}")
-            if a % 2 == 0:
+            for h in range(2):
+                cols = slice(h * HALF, (h + 1) * HALF)
                 nc.vector.tensor_scalar(
-                    result[:],
-                    windows[a][:],
+                    result[:, cols],
+                    windows[a][:, cols],
                     gain[:, a : a + 1],
                     shift[:, a : a + 1],
                     mybir.AluOpType.mult,
                     mybir.AluOpType.add,
                 )
-            else:
-                nc.scalar.activation(
-                    result[:],
-                    windows[a][:],
-                    mybir.ActivationFunctionType.Identity,
-                    bias=shift[:, a : a + 1],
-                    scale=gain[:, a : a + 1],
-                )
-            nc.sync.dma_start(out_blocks[a], result[:])
+                queue = nc.sync if h == 0 else nc.scalar
+                queue.dma_start(out_blocks[a][:, cols], result[:, cols])

@@ -11,6 +11,7 @@ S = 512
 N = 384
 BLOCKS = M // P
 HALF = S // 2
+WARM = 4
 
 FLOPS = 2 * P * M * N
 
@@ -24,6 +25,18 @@ def tile_scatter_matmul_kernel(tc, base, x, w, s, b, offs, out):
         tc.tile_pool(name="held", bufs=1) as held,
         tc.psum_pool(name="psum", bufs=1) as psum,
     ):
+        zeros = held.tile([P, P], BF16, name="zeros")
+        nc.gpsimd.memset(zeros[:], 0.0)
+        idle_bank = psum.tile([P, S // P, P], F32, name="idle_bank")
+        for i in range(WARM):
+            nc.tensor.matmul(
+                idle_bank[:],
+                zeros[:],
+                zeros[:].unsqueeze(1).to_broadcast([P, S // P, P]),
+                start=True,
+                stop=True,
+            )
+
         offsets = held.tile([P, N // 16], U16, name="offsets")
         nc.sync.dma_start(offsets[:], offs)
 

@@ -55,6 +55,9 @@ def tile_scatter_matmul_kernel(tc, base, x, w, s, b, offs, out):
             nc.sync.dma_start(gain[:], s.rearrange("(a p) o -> p (a o)", p=P))
             nc.scalar.dma_start(shift[:], b.rearrange("(a p) o -> p (a o)", p=P))
 
+        early = held.tile([P, 1], F32, name="early")
+        nc.scalar.activation(early[:], zeros[:, 0:1], mybir.ActivationFunctionType.Identity)
+
         ident = held.tile([P, P], BF16, name="ident")
         make_identity(nc, ident[:])
 
@@ -75,13 +78,22 @@ def tile_scatter_matmul_kernel(tc, base, x, w, s, b, offs, out):
             result = held.tile([P, S], F32, name=f"result{a}")
             for h in range(2):
                 cols = slice(h * HALF, (h + 1) * HALF)
-                nc.vector.tensor_scalar(
-                    result[:, cols],
-                    windows[a][:, cols],
-                    gain[:, a : a + 1],
-                    shift[:, a : a + 1],
-                    mybir.AluOpType.mult,
-                    mybir.AluOpType.add,
-                )
-                queue = nc.sync if h == 0 else nc.scalar
-                queue.dma_start(out_blocks[a][:, cols], result[:, cols])
+                if a % 2 == 0:
+                    nc.vector.tensor_scalar(
+                        result[:, cols],
+                        windows[a][:, cols],
+                        gain[:, a : a + 1],
+                        shift[:, a : a + 1],
+                        mybir.AluOpType.mult,
+                        mybir.AluOpType.add,
+                    )
+                    nc.sync.dma_start(out_blocks[a][:, cols], result[:, cols])
+                else:
+                    nc.scalar.activation(
+                        result[:, cols],
+                        windows[a][:, cols],
+                        mybir.ActivationFunctionType.Identity,
+                        bias=shift[:, a : a + 1],
+                        scale=gain[:, a : a + 1],
+                    )
+                    nc.scalar.dma_start(out_blocks[a][:, cols], result[:, cols])

@@ -79,6 +79,14 @@ def tile_scatter_matmul_kernel(tc, base, x, w, s, b, offs, out):
             for h in range(2):
                 cols = slice(h * HALF, (h + 1) * HALF)
                 if a % 2 == 0:
+                    nc.scalar.activation(
+                        result[:, cols],
+                        windows[a][:, cols],
+                        mybir.ActivationFunctionType.Identity,
+                        bias=shift[:, a : a + 1],
+                        scale=gain[:, a : a + 1],
+                    )
+                else:
                     nc.vector.tensor_scalar(
                         result[:, cols],
                         windows[a][:, cols],
@@ -87,13 +95,4 @@ def tile_scatter_matmul_kernel(tc, base, x, w, s, b, offs, out):
                         mybir.AluOpType.mult,
                         mybir.AluOpType.add,
                     )
-                    nc.sync.dma_start(out_blocks[a][:, cols], result[:, cols])
-                else:
-                    nc.scalar.activation(
-                        result[:, cols],
-                        windows[a][:, cols],
-                        mybir.ActivationFunctionType.Identity,
-                        bias=shift[:, a : a + 1],
-                        scale=gain[:, a : a + 1],
-                    )
-                    nc.scalar.dma_start(out_blocks[a][:, cols], result[:, cols])
+                nc.sync.dma_start(out_blocks[a][:, cols], result[:, cols])

@@ -10,7 +10,6 @@ M = 512
 S = 512
 N = 384
 BLOCKS = M // P
-HALF = S // 2
 WARM = 4
 
 FLOPS = 2 * P * M * N
@@ -76,23 +75,21 @@ def tile_scatter_matmul_kernel(tc, base, x, w, s, b, offs, out):
 
         for a in range(BLOCKS):
             result = held.tile([P, S], F32, name=f"result{a}")
-            for h in range(2):
-                cols = slice(h * HALF, (h + 1) * HALF)
-                if a % 2 == 0:
-                    nc.scalar.activation(
-                        result[:, cols],
-                        windows[a][:, cols],
-                        mybir.ActivationFunctionType.Identity,
-                        bias=shift[:, a : a + 1],
-                        scale=gain[:, a : a + 1],
-                    )
-                else:
-                    nc.vector.tensor_scalar(
-                        result[:, cols],
-                        windows[a][:, cols],
-                        gain[:, a : a + 1],
-                        shift[:, a : a + 1],
-                        mybir.AluOpType.mult,
-                        mybir.AluOpType.add,
-                    )
-                nc.sync.dma_start(out_blocks[a][:, cols], result[:, cols])
+            if a % 2 == 0:
+                nc.scalar.activation(
+                    result[:],
+                    windows[a][:],
+                    mybir.ActivationFunctionType.Identity,
+                    bias=shift[:, a : a + 1],
+                    scale=gain[:, a : a + 1],
+                )
+            else:
+                nc.vector.tensor_scalar(
+                    result[:],
+                    windows[a][:],
+                    gain[:, a : a + 1],
+                    shift[:, a : a + 1],
+                    mybir.AluOpType.mult,
+                    mybir.AluOpType.add,
+                )
+            nc.sync.dma_start(out_blocks[a], result[:])

@@ -17,8 +17,8 @@ FLOPS = 2 * P * M * N
 
 def tile_scatter_matmul_kernel(tc, base, x, w, s, b, offs, out):
     nc = tc.nc
-    base_blocks = base.rearrange("(a p) t -> a p t", p=P)
-    out_blocks = out.rearrange("(a p) t -> a p t", p=P)
+    base_blocks = base.rearrange("(p a) t -> a p t", a=BLOCKS)
+    out_blocks = out.rearrange("(p a) t -> a p t", a=BLOCKS)
 
     with (
         tc.tile_pool(name="held", bufs=1) as held,
@@ -50,9 +50,11 @@ def tile_scatter_matmul_kernel(tc, base, x, w, s, b, offs, out):
 
         gain = held.tile([P, BLOCKS], F32, name="gain")
         shift = held.tile([P, BLOCKS], F32, name="shift")
-        with nc.allow_non_contiguous_dma(reason="one float32 to a partition, 4 columns"):
-            nc.sync.dma_start(gain[:], s.rearrange("(a p) o -> p (a o)", p=P))
-            nc.scalar.dma_start(shift[:], b.rearrange("(a p) o -> p (a o)", p=P))
+        nc.sync.dma_start(gain[:], s.rearrange("(p a) o -> p (a o)", a=BLOCKS))
+        nc.scalar.dma_start(shift[:], b.rearrange("(p a) o -> p (a o)", a=BLOCKS))
+
+        w_blocks = held.tile([P, BLOCKS, P], BF16, name="w_blocks")
+        nc.vector.tensor_copy(w_blocks[:], w_tile[:].rearrange("k (p a) -> k a p", a=BLOCKS))
 
         early = held.tile([P, 1], F32, name="early")
         nc.scalar.activation(early[:], zeros[:, 0:1], mybir.ActivationFunctionType.Identity)
@@ -67,7 +69,7 @@ def tile_scatter_matmul_kernel(tc, base, x, w, s, b, offs, out):
         for a in range(BLOCKS):
             nc.tensor.matmul(
                 windows[a][:].indirect(offsets[:]),
-                w_tile[:, a * P : (a + 1) * P],
+                w_blocks[:, a, :],
                 x_tile[:],
                 start=False,
                 stop=True,

@@ -17,7 +17,7 @@ FLOPS = 2 * P * M * N
 
 def tile_scatter_matmul_kernel(tc, base, x, w, s, b, offs, out):
     nc = tc.nc
-    base_blocks = base.rearrange("(p a) t -> a p t", a=BLOCKS)
+    base_rows = base.rearrange("(p a) t -> p a t", a=BLOCKS)
     out_blocks = out.rearrange("(p a) t -> a p t", a=BLOCKS)
 
     with (
@@ -36,25 +36,25 @@ def tile_scatter_matmul_kernel(tc, base, x, w, s, b, offs, out):
                 stop=True,
             )
 
+        base_pairs = [held.tile([P, 2, S], BF16, name=f"base_pair{i}") for i in range(BLOCKS // 2)]
+        for i in range(BLOCKS // 2):
+            nc.sync.dma_start(base_pairs[i][:], base_rows[:, 2 * i : 2 * i + 2, :])
+        w_tile = held.tile([P, M], BF16, name="w_tile")
+        nc.sync.dma_start(w_tile[:], w)
         offsets = held.tile([P, N // 16], U16, name="offsets")
         nc.sync.dma_start(offsets[:], offs)
-
-        base_tiles = [held.tile([P, S], BF16, name=f"base{a}") for a in range(BLOCKS)]
-        for a in range(BLOCKS):
-            queue = nc.sync if a % 2 == 0 else nc.scalar
-            queue.dma_start(base_tiles[a][:], base_blocks[a])
         x_tile = held.tile([P, N], BF16, name="x_tile")
         nc.sync.dma_start(x_tile[:], x)
-        w_tile = held.tile([P, M], BF16, name="w_tile")
-        nc.scalar.dma_start(w_tile[:], w)
 
         gain = held.tile([P, BLOCKS], F32, name="gain")
         shift = held.tile([P, BLOCKS], F32, name="shift")
         nc.sync.dma_start(gain[:], s.rearrange("(p a) o -> p (a o)", a=BLOCKS))
-        nc.scalar.dma_start(shift[:], b.rearrange("(p a) o -> p (a o)", a=BLOCKS))
+        nc.sync.dma_start(shift[:], b.rearrange("(p a) o -> p (a o)", a=BLOCKS))
 
-        w_blocks = held.tile([P, BLOCKS, P], BF16, name="w_blocks")
-        nc.vector.tensor_copy(w_blocks[:], w_tile[:].rearrange("k (p a) -> k a p", a=BLOCKS))
+        w_columns = w_tile[:].rearrange("k (p a) -> k a p", a=BLOCKS)
+        w_blocks = [held.tile([P, P], BF16, name=f"w_block{a}") for a in range(BLOCKS)]
+        for a in range(BLOCKS):
+            nc.vector.tensor_copy(w_blocks[a][:], w_columns[:, a, :])
 
         early = held.tile([P, 1], F32, name="early")
         nc.scalar.activation(early[:], zeros[:, 0:1], mybir.ActivationFunctionType.Identity)
@@ -64,12 +64,12 @@ def tile_scatter_matmul_kernel(tc, base, x, w, s, b, offs, out):
 
         windows = [psum.tile([P, S], F32, name=f"window{a}") for a in range(BLOCKS)]
         for a in range(BLOCKS):
-            nc.tensor.matmul(windows[a][:], ident[:], base_tiles[a][:], start=True, stop=False)
+            nc.tensor.matmul(windows[a][:], ident[:], base_pairs[a // 2][:, a % 2, :], start=True, stop=False)
 
         for a in range(BLOCKS):
             nc.tensor.matmul(
                 windows[a][:].indirect(offsets[:]),
-                w_blocks[:, a, :],
+                w_blocks[a][:],
                 x_tile[:],
                 start=False,
                 stop=True,

@@ -17,8 +17,8 @@ FLOPS = 2 * P * M * N
 
 def tile_scatter_matmul_kernel(tc, base, x, w, s, b, offs, out):
     nc = tc.nc
-    base_rows = base.rearrange("(p a) t -> p a t", a=BLOCKS)
-    out_blocks = out.rearrange("(p a) t -> a p t", a=BLOCKS)
+    base_rows = base.rearrange("(i p j) t -> i p j t", i=2, j=2)
+    out_rows = out.rearrange("(i p j) t -> i j p t", i=2, j=2)
 
     with (
         tc.tile_pool(name="held", bufs=1) as held,
@@ -36,11 +36,11 @@ def tile_scatter_matmul_kernel(tc, base, x, w, s, b, offs, out):
                 stop=True,
             )
 
-        base_pairs = [held.tile([P, 2, S], BF16, name=f"base_pair{i}") for i in range(BLOCKS // 2)]
-        for i in range(BLOCKS // 2):
-            nc.sync.dma_start(base_pairs[i][:], base_rows[:, 2 * i : 2 * i + 2, :])
-        w_tile = held.tile([P, M], BF16, name="w_tile")
-        nc.sync.dma_start(w_tile[:], w)
+        base_pairs = [held.tile([P, 2, S], BF16, name=f"base_pair{i}") for i in range(2)]
+        w_halves = [held.tile([P, M // 2], BF16, name=f"w_half{i}") for i in range(2)]
+        for i in range(2):
+            nc.sync.dma_start(base_pairs[i][:], base_rows[i])
+        nc.sync.dma_start(w_halves[0][:], w[:, 0 : M // 2])
         offsets = held.tile([P, N // 16], U16, name="offsets")
         nc.sync.dma_start(offsets[:], offs)
         x_tile = held.tile([P, N], BF16, name="x_tile")
@@ -48,13 +48,18 @@ def tile_scatter_matmul_kernel(tc, base, x, w, s, b, offs, out):
 
         gain = held.tile([P, BLOCKS], F32, name="gain")
         shift = held.tile([P, BLOCKS], F32, name="shift")
-        nc.sync.dma_start(gain[:], s.rearrange("(p a) o -> p (a o)", a=BLOCKS))
-        nc.sync.dma_start(shift[:], b.rearrange("(p a) o -> p (a o)", a=BLOCKS))
+        nc.sync.dma_start(
+            gain[:].rearrange("p (i j) -> p i j", i=2), s.rearrange("(i p j) o -> p i (j o)", i=2, j=2)
+        )
+        nc.sync.dma_start(
+            shift[:].rearrange("p (i j) -> p i j", i=2), b.rearrange("(i p j) o -> p i (j o)", i=2, j=2)
+        )
+        nc.sync.dma_start(w_halves[1][:], w[:, M // 2 : M])
 
-        w_columns = w_tile[:].rearrange("k (p a) -> k a p", a=BLOCKS)
         w_blocks = [held.tile([P, P], BF16, name=f"w_block{a}") for a in range(BLOCKS)]
         for a in range(BLOCKS):
-            nc.vector.tensor_copy(w_blocks[a][:], w_columns[:, a, :])
+            w_columns = w_halves[a // 2][:].rearrange("k (p j) -> k j p", j=2)
+            nc.vector.tensor_copy(w_blocks[a][:], w_columns[:, a % 2, :])
 
         early = held.tile([P, 1], F32, name="early")
         nc.scalar.activation(early[:], zeros[:, 0:1], mybir.ActivationFunctionType.Identity)
@@ -94,4 +99,4 @@ def tile_scatter_matmul_kernel(tc, base, x, w, s, b, offs, out):
                     mybir.AluOpType.mult,
                     mybir.AluOpType.add,
                 )
-            nc.sync.dma_start(out_blocks[a], result[:])
+            nc.sync.dma_start(out_rows[a // 2, a % 2], result[:])

@@ -82,21 +82,25 @@ def tile_scatter_matmul_kernel(tc, base, x, w, s, b, offs, out):
 
         for a in range(BLOCKS):
             result = held.tile([P, S], F32, name=f"result{a}")
-            if a % 2 == 0:
-                nc.scalar.activation(
-                    result[:],
-                    windows[a][:],
-                    mybir.ActivationFunctionType.Identity,
-                    bias=shift[:, a : a + 1],
-                    scale=gain[:, a : a + 1],
-                )
-            else:
-                nc.vector.tensor_scalar(
-                    result[:],
-                    windows[a][:],
-                    gain[:, a : a + 1],
-                    shift[:, a : a + 1],
-                    mybir.AluOpType.mult,
-                    mybir.AluOpType.add,
-                )
-            nc.sync.dma_start(out_rows[a // 2, a % 2], result[:])
+            pieces = 2 if a == 0 else 1
+            width = S // pieces
+            for h in range(pieces):
+                cols = slice(h * width, (h + 1) * width)
+                if a % 2 == 0:
+                    nc.scalar.activation(
+                        result[:, cols],
+                        windows[a][:, cols],
+                        mybir.ActivationFunctionType.Identity,
+                        bias=shift[:, a : a + 1],
+                        scale=gain[:, a : a + 1],
+                    )
+                else:
+                    nc.vector.tensor_scalar(
+                        result[:, cols],
+                        windows[a][:, cols],
+                        gain[:, a : a + 1],
+                        shift[:, a : a + 1],
+                        mybir.AluOpType.mult,
+                        mybir.AluOpType.add,
+                    )
+                nc.sync.dma_start(out_rows[a // 2, a % 2][:, cols], result[:, cols])

@@ -10,6 +10,9 @@ M = 512
 S = 512
 N = 384
 BLOCKS = M // P
+RUN = 2
+PIECES = 12
+PIECE = 44
 WARM = 4
 
 FLOPS = 2 * P * M * N
@@ -38,8 +41,7 @@ def tile_scatter_matmul_kernel(tc, base, x, w, s, b, offs, out):
 
         base_pairs = [held.tile([P, 2, S], BF16, name=f"base_pair{i}") for i in range(2)]
         w_halves = [held.tile([P, M // 2], BF16, name=f"w_half{i}") for i in range(2)]
-        for i in range(2):
-            nc.sync.dma_start(base_pairs[i][:], base_rows[i])
+        nc.sync.dma_start(base_pairs[0][:], base_rows[0])
         nc.sync.dma_start(w_halves[0][:], w[:, 0 : M // 2])
         offsets = held.tile([P, N // 16], U16, name="offsets")
         nc.sync.dma_start(offsets[:], offs)
@@ -55,6 +57,7 @@ def tile_scatter_matmul_kernel(tc, base, x, w, s, b, offs, out):
             shift[:].rearrange("p (i j) -> p i j", i=2), b.rearrange("(i p j) o -> p i (j o)", i=2, j=2)
         )
         nc.sync.dma_start(w_halves[1][:], w[:, M // 2 : M])
+        nc.sync.dma_start(base_pairs[1][:], base_rows[1])
 
         w_blocks = [held.tile([P, P], BF16, name=f"w_block{a}") for a in range(BLOCKS)]
         for a in range(BLOCKS):
@@ -68,17 +71,18 @@ def tile_scatter_matmul_kernel(tc, base, x, w, s, b, offs, out):
         make_identity(nc, ident[:])
 
         windows = [psum.tile([P, S], F32, name=f"window{a}") for a in range(BLOCKS)]
-        for a in range(BLOCKS):
-            nc.tensor.matmul(windows[a][:], ident[:], base_pairs[a // 2][:, a % 2, :], start=True, stop=False)
-
-        for a in range(BLOCKS):
-            nc.tensor.matmul(
-                windows[a][:].indirect(offsets[:]),
-                w_blocks[a][:],
-                x_tile[:],
-                start=False,
-                stop=True,
-            )
+        for a in range(RUN):
+            nc.tensor.matmul(windows[a][:], ident[:], base_pairs[0][:, a, :], start=True, stop=False)
+        for a in range(RUN):
+            nc.tensor.matmul(windows[a][:].indirect(offsets[:]), w_blocks[a][:], x_tile[:], start=False, stop=True)
+        for a in range(RUN, BLOCKS):
+            for i in range(PIECES):
+                cols = slice(i * PIECE, min((i + 1) * PIECE, S))
+                nc.tensor.matmul(
+                    windows[a][:, cols], ident[:], base_pairs[1][:, a - RUN, cols], start=i == 0, stop=False
+                )
+        for a in range(RUN, BLOCKS):
+            nc.tensor.matmul(windows[a][:].indirect(offsets[:]), w_blocks[a][:], x_tile[:], start=False, stop=True)
 
         for a in range(BLOCKS):
             result = held.tile([P, S], F32, name=f"result{a}")

@@ -86,7 +86,7 @@ def tile_scatter_matmul_kernel(tc, base, x, w, s, b, offs, out):
 
         for a in range(BLOCKS):
             result = held.tile([P, S], F32, name=f"result{a}")
-            pieces = 2 if a == 0 else 1
+            pieces = 1 if a < RUN else 2
             width = S // pieces
             for h in range(pieces):
                 cols = slice(h * width, (h + 1) * width)

@@ -13,7 +13,7 @@ BLOCKS = M // P
 RUN = 2
 PIECES = 12
 PIECE = 44
-WARM = 4
+WARM = 3
 
 FLOPS = 2 * P * M * N
 

@@ -56,8 +56,8 @@ def tile_scatter_matmul_kernel(tc, base, x, w, s, b, offs, out):
         nc.sync.dma_start(
             shift[:].rearrange("p (i j) -> p i j", i=2), b.rearrange("(i p j) o -> p i (j o)", i=2, j=2)
         )
-        nc.sync.dma_start(w_halves[1][:], w[:, M // 2 : M])
         nc.sync.dma_start(base_pairs[1][:], base_rows[1])
+        nc.sync.dma_start(w_halves[1][:], w[:, M // 2 : M])
 
         w_blocks = [held.tile([P, P], BF16, name=f"w_block{a}") for a in range(BLOCKS)]
         for a in range(BLOCKS):

@@ -39,9 +39,11 @@ def tile_scatter_matmul_kernel(tc, base, x, w, s, b, offs, out):
                 stop=True,
             )
 
-        base_pairs = [held.tile([P, 2, S], BF16, name=f"base_pair{i}") for i in range(2)]
+        base_first = [held.tile([P, S], BF16, name=f"base_first{j}") for j in range(RUN)]
+        base_second = held.tile([P, 2, S], BF16, name="base_second")
         w_halves = [held.tile([P, M // 2], BF16, name=f"w_half{i}") for i in range(2)]
-        nc.sync.dma_start(base_pairs[0][:], base_rows[0])
+        for j in range(RUN):
+            nc.sync.dma_start(base_first[j][:], base_rows[0, :, j, :])
         nc.sync.dma_start(w_halves[0][:], w[:, 0 : M // 2])
         offsets = held.tile([P, N // 16], U16, name="offsets")
         nc.sync.dma_start(offsets[:], offs)
@@ -56,7 +58,7 @@ def tile_scatter_matmul_kernel(tc, base, x, w, s, b, offs, out):
         nc.sync.dma_start(
             shift[:].rearrange("p (i j) -> p i j", i=2), b.rearrange("(i p j) o -> p i (j o)", i=2, j=2)
         )
-        nc.sync.dma_start(base_pairs[1][:], base_rows[1])
+        nc.sync.dma_start(base_second[:], base_rows[1])
         nc.sync.dma_start(w_halves[1][:], w[:, M // 2 : M])
 
         w_blocks = [held.tile([P, P], BF16, name=f"w_block{a}") for a in range(BLOCKS)]
@@ -72,14 +74,14 @@ def tile_scatter_matmul_kernel(tc, base, x, w, s, b, offs, out):
 
         windows = [psum.tile([P, S], F32, name=f"window{a}") for a in range(BLOCKS)]
         for a in range(RUN):
-            nc.tensor.matmul(windows[a][:], ident[:], base_pairs[0][:, a, :], start=True, stop=False)
+            nc.tensor.matmul(windows[a][:], ident[:], base_first[a][:], start=True, stop=False)
         for a in range(RUN):
             nc.tensor.matmul(windows[a][:].indirect(offsets[:]), w_blocks[a][:], x_tile[:], start=False, stop=True)
         for a in range(RUN, BLOCKS):
             for i in range(PIECES):
                 cols = slice(i * PIECE, min((i + 1) * PIECE, S))
                 nc.tensor.matmul(
-                    windows[a][:, cols], ident[:], base_pairs[1][:, a - RUN, cols], start=i == 0, stop=False
+                    windows[a][:, cols], ident[:], base_second[:, a - RUN, cols], start=i == 0, stop=False
                 )
         for a in range(RUN, BLOCKS):
             nc.tensor.matmul(windows[a][:].indirect(offsets[:]), w_blocks[a][:], x_tile[:], start=False, stop=True)

@@ -58,8 +58,8 @@ def tile_scatter_matmul_kernel(tc, base, x, w, s, b, offs, out):
         nc.sync.dma_start(
             shift[:].rearrange("p (i j) -> p i j", i=2), b.rearrange("(i p j) o -> p i (j o)", i=2, j=2)
         )
-        nc.sync.dma_start(base_second[:], base_rows[1])
         nc.sync.dma_start(w_halves[1][:], w[:, M // 2 : M])
+        nc.sync.dma_start(base_second[:], base_rows[1])
 
         w_blocks = [held.tile([P, P], BF16, name=f"w_block{a}") for a in range(BLOCKS)]
         for a in range(BLOCKS):

import concourse.mybir as mybir
from concourse.masks import make_identity

BF16 = mybir.dt.bfloat16
F32 = mybir.dt.float32
U16 = mybir.dt.uint16

P = 128
M = 512
S = 512
N = 384
BLOCKS = M // P
RUN = 2
PIECES = 12
PIECE = 44
WARM = 3

FLOPS = 2 * P * M * N


def tile_scatter_matmul_kernel(tc, base, x, w, s, b, offs, out):
    nc = tc.nc
    base_rows = base.rearrange("(i p j) t -> i p j t", i=2, j=2)
    out_rows = out.rearrange("(i p j) t -> i j p t", i=2, j=2)

    with (
        tc.tile_pool(name="held", bufs=1) as held,
        tc.psum_pool(name="psum", bufs=1) as psum,
    ):
        zeros = held.tile([P, P], BF16, name="zeros")
        nc.gpsimd.memset(zeros[:], 0.0)
        idle_bank = psum.tile([P, S // P, P], F32, name="idle_bank")
        for i in range(WARM):
            nc.tensor.matmul(
                idle_bank[:],
                zeros[:],
                zeros[:].unsqueeze(1).to_broadcast([P, S // P, P]),
                start=True,
                stop=True,
            )

        base_first = [held.tile([P, S], BF16, name=f"base_first{j}") for j in range(RUN)]
        base_second = held.tile([P, 2, S], BF16, name="base_second")
        w_halves = [held.tile([P, M // 2], BF16, name=f"w_half{i}") for i in range(2)]
        for j in range(RUN):
            nc.sync.dma_start(base_first[j][:], base_rows[0, :, j, :])
        nc.sync.dma_start(w_halves[0][:], w[:, 0 : M // 2])
        offsets = held.tile([P, N // 16], U16, name="offsets")
        nc.sync.dma_start(offsets[:], offs)
        x_tile = held.tile([P, N], BF16, name="x_tile")
        nc.sync.dma_start(x_tile[:], x)

        gain = held.tile([P, BLOCKS], F32, name="gain")
        shift = held.tile([P, BLOCKS], F32, name="shift")
        nc.sync.dma_start(
            gain[:].rearrange("p (i j) -> p i j", i=2), s.rearrange("(i p j) o -> p i (j o)", i=2, j=2)
        )
        nc.sync.dma_start(
            shift[:].rearrange("p (i j) -> p i j", i=2), b.rearrange("(i p j) o -> p i (j o)", i=2, j=2)
        )
        nc.sync.dma_start(w_halves[1][:], w[:, M // 2 : M])
        nc.sync.dma_start(base_second[:], base_rows[1])

        w_blocks = [held.tile([P, P], BF16, name=f"w_block{a}") for a in range(BLOCKS)]
        for a in range(BLOCKS):
            w_columns = w_halves[a // 2][:].rearrange("k (p j) -> k j p", j=2)
            nc.vector.tensor_copy(w_blocks[a][:], w_columns[:, a % 2, :])

        early = held.tile([P, 1], F32, name="early")
        nc.scalar.activation(early[:], zeros[:, 0:1], mybir.ActivationFunctionType.Identity)

        ident = held.tile([P, P], BF16, name="ident")
        make_identity(nc, ident[:])

        windows = [psum.tile([P, S], F32, name=f"window{a}") for a in range(BLOCKS)]
        for a in range(RUN):
            nc.tensor.matmul(windows[a][:], ident[:], base_first[a][:], start=True, stop=False)
        for a in range(RUN):
            nc.tensor.matmul(windows[a][:].indirect(offsets[:]), w_blocks[a][:], x_tile[:], start=False, stop=True)
        for a in range(RUN, BLOCKS):
            for i in range(PIECES):
                cols = slice(i * PIECE, min((i + 1) * PIECE, S))
                nc.tensor.matmul(
                    windows[a][:, cols], ident[:], base_second[:, a - RUN, cols], start=i == 0, stop=False
                )
        for a in range(RUN, BLOCKS):
            nc.tensor.matmul(windows[a][:].indirect(offsets[:]), w_blocks[a][:], x_tile[:], start=False, stop=True)

        for a in range(BLOCKS):
            result = held.tile([P, S], F32, name=f"result{a}")
            pieces = 1 if a < RUN else 2
            width = S // pieces
            for h in range(pieces):
                cols = slice(h * width, (h + 1) * width)
                if a % 2 == 0:
                    nc.scalar.activation(
                        result[:, cols],
                        windows[a][:, cols],
                        mybir.ActivationFunctionType.Identity,
                        bias=shift[:, a : a + 1],
                        scale=gain[:, a : a + 1],
                    )
                else:
                    nc.vector.tensor_scalar(
                        result[:, cols],
                        windows[a][:, cols],
                        gain[:, a : a + 1],
                        shift[:, a : a + 1],
                        mybir.AluOpType.mult,
                        mybir.AluOpType.add,
                    )
                nc.sync.dma_start(out_rows[a // 2, a % 2][:, cols], result[:, cols])
